import numpy as np
import ml_dtypes


def mxq(x, axis, fmt="e4m3"):
    dtype, down = {"e4m3": (ml_dtypes.float8_e4m3fn, 7), "e5m2": (ml_dtypes.float8_e5m2, 14)}[fmt]
    v = np.moveaxis(np.asarray(x, np.float32).astype(ml_dtypes.bfloat16).astype(np.float64), axis, -1)
    blocks = v.reshape(v.shape[:-1] + (-1, 32))
    amax = np.abs(blocks).max(-1, keepdims=True)
    byte = np.maximum(np.where(amax > 0, np.frexp(amax)[1] - 1 + 127, 0) - down, 1)
    scale = np.exp2(byte - 127.0)
    codes = (blocks / scale).astype(np.float32).astype(dtype).astype(np.float64)
    return np.moveaxis((codes * scale).reshape(v.shape), -1, axis)


WIDE = False


def mx_kscale(k):
    if not WIDE:
        return np.ones(k)
    levels = np.array([10, -10, 5, -5, 0])
    if k % 512:
        return np.exp2(np.random.permutation(np.resize(levels, k // 32))).repeat(32)
    a = np.empty((k // 512, 16))
    for p in range(k // 512):
        a[p, :8] = np.random.permutation(np.resize(levels, 8))
        for g in range(8):
            far = levels[np.abs(levels - a[p, g]) >= 10]
            a[p, g + 8] = far[np.random.randint(len(far))]
    return np.exp2(a.ravel()).repeat(32)


def f64(x):
    return np.asarray(x).astype(np.float64)


def striped(idx):
    return np.tile(idx.reshape(-1, 16).T, (8, 1)).astype(np.uint16)


def unstriped(offs):
    return offs[:16].T.reshape(-1).astype(np.int64)


E2M1 = np.array([0.0, 0.5, 1.0, 1.5, 2.0, 3.0, 4.0, 6.0, -0.0, -0.5, -1.0, -1.5, -2.0, -3.0, -4.0, -6.0])


def pack_fp4(w):
    k, n = w.shape
    w = f64(np.asarray(w, np.float32).astype(ml_dtypes.bfloat16)).reshape(k // 32, 32, n)
    amax = np.abs(w).max(1)
    mant, ex = np.frexp(amax / 6.0)
    byte = np.clip(np.where(amax > 0, np.where(mant > 0.5, ex, ex - 1) + 127, 1), 1, 254)
    scaled = (w * np.exp2(127.0 - byte)[:, None, :]).reshape(k, n).astype(np.float32)
    c = np.ascontiguousarray(scaled.reshape(k // 512, 128, 4, n).transpose(0, 1, 3, 2)).astype(ml_dtypes.float4_e2m1fn).view(np.uint8) & 0xF
    words = (c[..., 0::2] | (c[..., 1::2] << 4)).reshape(k // 512, 128, 2 * n)
    return np.ascontiguousarray(words), np.ascontiguousarray(byte.astype(np.uint8).reshape(k // 512, 16, n))


def unpack_fp4(words, scales):
    g, _, n = scales.shape
    words = np.ascontiguousarray(words).reshape(g, 128, n, 2)
    nib = np.empty((g, 128, n, 4), np.uint8)
    nib[..., 0::2] = words & 0xF
    nib[..., 1::2] = words >> 4
    vals = E2M1[nib] * np.repeat(np.exp2(scales.astype(np.float64) - 127.0), 8, axis=1)[..., None]
    return vals.transpose(0, 1, 3, 2).reshape(g * 512, n)


K, T, S, N = 512, 2048, 1024, 128


def setup_inputs():
    n = np.random.standard_normal
    s = mx_kscale(K)[:, None]
    packed_w1 = pack_fp4(n((K, N)) / np.sqrt(K) / s)
    return {
        "xT": (n((K, T)) * s).astype(np.float32),
        "w1_words": packed_w1[0],
        "w1_scales": packed_w1[1],
        "offs": striped(np.random.permutation(T)[:S]),
    }


def reference(xT, w1_words, w1_scales, offs):
    xq = mxq(f64(xT)[:, unstriped(offs)], 0, "e4m3")
    y = unpack_fp4(w1_words, w1_scales).T @ xq
    e = np.exp(y - y.max(axis=1, keepdims=True))
    return e / e.sum(axis=1, keepdims=True)

@@ -1,0 +1,169 @@
+from contextlib import ExitStack
+
+import concourse.mybir as mybir
+
+K, T, S, N = 512, 2048, 1024, 128
+FLOPS = 2 * K * S * N
+
+F32 = mybir.dt.float32
+BF16 = mybir.dt.bfloat16
+I32 = mybir.dt.int32
+U32 = mybir.dt.uint32
+U16 = mybir.dt.uint16
+U8 = mybir.dt.uint8
+FP8X4 = mybir.dt.float8_e4m3fn_x4
+FP4X4 = mybir.dt.float4_e2m1fn_x4
+ALU = mybir.AluOpType
+ACT = mybir.ActivationFunctionType
+
+P = 128
+CHUNK = 256
+CHUNKS = S // CHUNK
+LOADS = (
+    ((1024, 1024), (1024, 672)),
+    ((1024, 256), (512, 512), (256, 256), (256, 176)),
+)
+
+
+def tile_picked_rank_none_e_kernel(tc, xT, w1_words, w1_scales, offs, out):
+    nc = tc.nc
+    with ExitStack() as ctx:
+        sb = ctx.enter_context(tc.tile_pool(name="sb", bufs=1))
+        ps = ctx.enter_context(tc.psum_pool(name="ps", bufs=1))
+
+        rows = xT.rearrange("(p j) t -> p j t", j=4)
+        offsets = sb.tile([P, S // 16], U16, name="offsets")
+        raw = []
+        for u in range(2):
+            t0 = 0
+            for i, (width, on_vector) in enumerate(LOADS[u]):
+                piece = sb.tile([P, 2, width], F32, name=f"raw{u}_{i}")
+                nc.sync.dma_start(out=piece[:], in_=rows[:, 2 * u : 2 * u + 2, t0 : t0 + width])
+                raw.append((u, t0, width, on_vector, piece))
+                t0 = t0 + width
+                if u == 0 and i == 0:
+                    nc.sync.dma_start(offsets[:], offs)
+
+        w_words = sb.tile([P, 2 * N], U8, name="w_words", align_bytes=64)
+        w_scales = sb.tile([P, N], U8, name="w_scales", align_bytes=64)
+        nc.gpsimd.memset(w_scales[:], 0)
+        nc.gpsimd.dma_start(out=w_words[:].bitcast(I32), in_=w1_words[0].bitcast(I32))
+        for q in range(4):
+            nc.gpsimd.dma_start(
+                out=w_scales[32 * q : 32 * q + 4, :].bitcast(I32),
+                in_=w1_scales[0, 4 * q : 4 * q + 4, :].bitcast(I32),
+            )
+
+        warm = sb.tile([P, 2], F32, name="warm")
+        nc.vector.memset(warm[:, 0:1], 0.0)
+        nc.scalar.activation(warm[:, 1:2], warm[:, 0:1], ACT.Exp)
+
+        pairs = [sb.tile([P, T, 2], BF16, name=f"pairs{u}") for u in range(2)]
+        picked = [sb.tile([P, 2, CHUNK], U32, name=f"picked{c}") for c in range(CHUNKS)]
+
+        def round_piece(u, t0, width, on_vector, piece):
+            nc.vector.tensor_copy(
+                out=pairs[u][:, t0 : t0 + on_vector, :],
+                in_=piece[:, :, 0:on_vector].rearrange("p e t -> p t e"),
+            )
+            if on_vector < width:
+                nc.scalar.activation(
+                    pairs[u][:, t0 + on_vector : t0 + width, :],
+                    piece[:, :, on_vector:width].rearrange("p e t -> p t e"),
+                    ACT.Copy,
+                )
+
+        def gather(u, c):
+            window = pairs[u][:].rearrange("p t e -> p (t e)").bitcast(U32)
+            cols = CHUNK // 16
+            nc.vector.tensor_copy(picked[c][:, u, :], window.indirect(offsets[:, c * cols : (c + 1) * cols]))
+
+        for item in raw:
+            if item[0] == 0:
+                round_piece(*item)
+        for c in range(CHUNKS):
+            gather(0, c)
+        for item in raw:
+            if item[0] == 1:
+                round_piece(*item)
+
+        woven = [sb.tile([P, 4 * CHUNK], BF16, name=f"woven{c}", align_bytes=64) for c in range(CHUNKS)]
+        codes = [sb.tile([P, CHUNK], U32, name=f"codes{c}", align_bytes=64) for c in range(CHUNKS)]
+        scales = [sb.tile([P, CHUNK], U8, name=f"scales{c}", align_bytes=64) for c in range(CHUNKS)]
+        scores = [ps.tile([P, CHUNK], F32, name=f"scores{c}") for c in range(CHUNKS)]
+        neg = [sb.tile([P, CHUNK], F32, name=f"neg{c}") for c in range(CHUNKS)]
+        expd = [sb.tile([P, CHUNK], F32, name=f"expd{c}") for c in range(CHUNKS)]
+        res = [sb.tile([P, CHUNK], F32, name=f"res{c}") for c in range(CHUNKS)]
+        negmax = sb.tile([P, CHUNKS], F32, name="negmax")
+        sums = sb.tile([P, CHUNKS], F32, name="sums")
+        fix = sb.tile([P, CHUNKS], F32, name="fix")
+        terms = sb.tile([P, CHUNKS], F32, name="terms")
+        total = sb.tile([P, 1], F32, name="total")
+        inv = sb.tile([P, 1], F32, name="inv")
+
+        def weave(c):
+            nc.scalar.copy(
+                woven[c][:].bitcast(U32).rearrange("p (s u) -> p s u", u=2),
+                picked[c][:].rearrange("p u s -> p s u"),
+            )
+
+        def product(c):
+            nc.vector.quantize_mx(out=codes[c][:].bitcast(FP8X4), scales=scales[c][:], in_=woven[c][:])
+            nc.tensor.matmul_mx(
+                scores[c][:],
+                lhsT=w_words[:].bitcast(FP4X4),
+                lhsT_scale=w_scales[:],
+                rhs=codes[c][:].bitcast(FP8X4),
+                rhs_scale=scales[c][:],
+                start=True,
+                stop=True,
+            )
+
+        def running_max(c):
+            nc.vector.tensor_scalar(
+                neg[c][:],
+                scores[c][:],
+                -1.0,
+                negmax[:, c - 1 : c] if c else None,
+                op0=ALU.mult,
+                op1=ALU.min,
+                accum_out=negmax[:, c : c + 1],
+            )
+
+        def exponent(c):
+            nc.scalar.activation(
+                expd[c][:], neg[c][:], ACT.Exp, bias=negmax[:, c : c + 1], scale=-1.0, accum_out=sums[:, c : c + 1]
+            )
+
+        last = CHUNKS - 1
+
+        def softmax_part(c):
+            running_max(c)
+            if c == last:
+                nc.scalar.activation(fix[:], negmax[:], ACT.Exp, bias=negmax[:, last:CHUNKS], scale=-1.0)
+            exponent(c)
+
+        for c in range(last):
+            gather(1, c)
+            weave(c)
+        product(0)
+        gather(1, last)
+        weave(last)
+        product(1)
+        product(2)
+        softmax_part(0)
+        product(3)
+        for c in range(1, CHUNKS):
+            softmax_part(c)
+
+        nc.vector.scalar_tensor_tensor(
+            terms[:], sums[:], 1.0, fix[:], op0=ALU.mult, op1=ALU.mult, accum_out=total[:]
+        )
+        nc.vector.reciprocal(inv[:], total[:])
+        for c in range(last):
+            nc.vector.tensor_scalar(
+                res[c][:], expd[c][:], fix[:, c : c + 1], inv[:], op0=ALU.mult, op1=ALU.mult
+            )
+            nc.sync.dma_start(out=out[:, c * CHUNK : (c + 1) * CHUNK], in_=res[c][:])
+        nc.scalar.activation(res[last][:], expd[last][:], ACT.Copy, scale=inv[:])
+        nc.scalar.dma_start(out=out[:, last * CHUNK : S], in_=res[last][:])

@@ -20,8 +20,8 @@ P = 128
 CHUNK = 256
 CHUNKS = S // CHUNK
 LOADS = (
-    ((1024, 1024), (1024, 672)),
-    ((1024, 256), (512, 512), (256, 256), (256, 176)),
+    ((1024, 680), (1024, 680)),
+    ((1024, 680), (512, 344), (256, 176), (256, 176)),
 )
 
 
@@ -33,23 +33,24 @@ def tile_picked_rank_none_e_kernel(tc, xT, w1_words, w1_scales, offs, out):
 
         rows = xT.rearrange("(p j) t -> p j t", j=4)
         offsets = sb.tile([P, S // 16], U16, name="offsets")
-        raw = []
+        raw = [sb.tile([P, 2, T], F32, name=f"raw{u}") for u in range(2)]
+        pieces = []
         for u in range(2):
+            nc.sync.dma_start(out=raw[u][:, 0, :], in_=rows[:, 2 * u, :])
             t0 = 0
-            for i, (width, on_vector) in enumerate(LOADS[u]):
-                piece = sb.tile([P, 2, width], F32, name=f"raw{u}_{i}")
-                nc.sync.dma_start(out=piece[:], in_=rows[:, 2 * u : 2 * u + 2, t0 : t0 + width])
-                raw.append((u, t0, width, on_vector, piece))
+            for width, on_vector in LOADS[u]:
+                nc.sync.dma_start(out=raw[u][:, 1, t0 : t0 + width], in_=rows[:, 2 * u + 1, t0 : t0 + width])
+                pieces.append((u, t0, width, on_vector))
                 t0 = t0 + width
-                if u == 0 and i == 0:
-                    nc.sync.dma_start(offsets[:], offs)
+            if u == 0:
+                nc.sync.dma_start(offsets[:], offs)
 
         w_words = sb.tile([P, 2 * N], U8, name="w_words", align_bytes=64)
         w_scales = sb.tile([P, N], U8, name="w_scales", align_bytes=64)
-        nc.gpsimd.memset(w_scales[:], 0)
-        nc.gpsimd.dma_start(out=w_words[:].bitcast(I32), in_=w1_words[0].bitcast(I32))
+        nc.vector.memset(w_scales[:].bitcast(I32), 0)
+        nc.sync.dma_start(out=w_words[:].bitcast(I32), in_=w1_words[0].bitcast(I32))
         for q in range(4):
-            nc.gpsimd.dma_start(
+            nc.sync.dma_start(
                 out=w_scales[32 * q : 32 * q + 4, :].bitcast(I32),
                 in_=w1_scales[0, 4 * q : 4 * q + 4, :].bitcast(I32),
             )
@@ -61,15 +62,15 @@ def tile_picked_rank_none_e_kernel(tc, xT, w1_words, w1_scales, offs, out):
         pairs = [sb.tile([P, T, 2], BF16, name=f"pairs{u}") for u in range(2)]
         picked = [sb.tile([P, 2, CHUNK], U32, name=f"picked{c}") for c in range(CHUNKS)]
 
-        def round_piece(u, t0, width, on_vector, piece):
+        def round_piece(u, t0, width, on_vector):
             nc.vector.tensor_copy(
                 out=pairs[u][:, t0 : t0 + on_vector, :],
-                in_=piece[:, :, 0:on_vector].rearrange("p e t -> p t e"),
+                in_=raw[u][:, :, t0 : t0 + on_vector].rearrange("p e t -> p t e"),
             )
             if on_vector < width:
                 nc.scalar.activation(
                     pairs[u][:, t0 + on_vector : t0 + width, :],
-                    piece[:, :, on_vector:width].rearrange("p e t -> p t e"),
+                    raw[u][:, :, t0 + on_vector : t0 + width].rearrange("p e t -> p t e"),
                     ACT.Copy,
                 )
 
@@ -78,12 +79,12 @@ def tile_picked_rank_none_e_kernel(tc, xT, w1_words, w1_scales, offs, out):
             cols = CHUNK // 16
             nc.vector.tensor_copy(picked[c][:, u, :], window.indirect(offsets[:, c * cols : (c + 1) * cols]))
 
-        for item in raw:
+        for item in pieces:
             if item[0] == 0:
                 round_piece(*item)
         for c in range(CHUNKS):
             gather(0, c)
-        for item in raw:
+        for item in pieces:
             if item[0] == 1:
                 round_piece(*item)
 
@@ -91,10 +92,10 @@ def tile_picked_rank_none_e_kernel(tc, xT, w1_words, w1_scales, offs, out):
         codes = [sb.tile([P, CHUNK], U32, name=f"codes{c}", align_bytes=64) for c in range(CHUNKS)]
         scales = [sb.tile([P, CHUNK], U8, name=f"scales{c}", align_bytes=64) for c in range(CHUNKS)]
         scores = [ps.tile([P, CHUNK], F32, name=f"scores{c}") for c in range(CHUNKS)]
-        neg = [sb.tile([P, CHUNK], F32, name=f"neg{c}") for c in range(CHUNKS)]
         expd = [sb.tile([P, CHUNK], F32, name=f"expd{c}") for c in range(CHUNKS)]
         res = [sb.tile([P, CHUNK], F32, name=f"res{c}") for c in range(CHUNKS)]
         negmax = sb.tile([P, CHUNKS], F32, name="negmax")
+        negtop = sb.tile([P, 1], F32, name="negtop")
         sums = sb.tile([P, CHUNKS], F32, name="sums")
         fix = sb.tile([P, CHUNKS], F32, name="fix")
         terms = sb.tile([P, CHUNKS], F32, name="terms")
@@ -119,30 +120,13 @@ def tile_picked_rank_none_e_kernel(tc, xT, w1_words, w1_scales, offs, out):
                 stop=True,
             )
 
-        def running_max(c):
-            nc.vector.tensor_scalar(
-                neg[c][:],
-                scores[c][:],
-                -1.0,
-                negmax[:, c - 1 : c] if c else None,
-                op0=ALU.mult,
-                op1=ALU.min,
-                accum_out=negmax[:, c : c + 1],
-            )
-
-        def exponent(c):
+        def softmax_part(c):
+            nc.vector.tensor_reduce(negmax[:, c : c + 1], scores[c][:], mybir.AxisListType.X, ALU.max, negate=True)
             nc.scalar.activation(
-                expd[c][:], neg[c][:], ACT.Exp, bias=negmax[:, c : c + 1], scale=-1.0, accum_out=sums[:, c : c + 1]
+                expd[c][:], scores[c][:], ACT.Exp, bias=negmax[:, c : c + 1], accum_out=sums[:, c : c + 1]
             )
 
         last = CHUNKS - 1
-
-        def softmax_part(c):
-            running_max(c)
-            if c == last:
-                nc.scalar.activation(fix[:], negmax[:], ACT.Exp, bias=negmax[:, last:CHUNKS], scale=-1.0)
-            exponent(c)
-
         for c in range(last):
             gather(1, c)
             weave(c)
@@ -156,14 +140,15 @@ def tile_picked_rank_none_e_kernel(tc, xT, w1_words, w1_scales, offs, out):
         for c in range(1, CHUNKS):
             softmax_part(c)
 
+        nc.vector.tensor_reduce(negtop[:], negmax[:], mybir.AxisListType.X, ALU.min)
+        nc.scalar.activation(fix[:], negmax[:], ACT.Exp, bias=negtop[:], scale=-1.0)
         nc.vector.scalar_tensor_tensor(
             terms[:], sums[:], 1.0, fix[:], op0=ALU.mult, op1=ALU.mult, accum_out=total[:]
         )
         nc.vector.reciprocal(inv[:], total[:])
-        for c in range(last):
+        for c in range(CHUNKS):
             nc.vector.tensor_scalar(
                 res[c][:], expd[c][:], fix[:, c : c + 1], inv[:], op0=ALU.mult, op1=ALU.mult
             )
-            nc.sync.dma_start(out=out[:, c * CHUNK : (c + 1) * CHUNK], in_=res[c][:])
-        nc.scalar.activation(res[last][:], expd[last][:], ACT.Copy, scale=inv[:])
-        nc.scalar.dma_start(out=out[:, last * CHUNK : S], in_=res[last][:])
+            queue = nc.scalar if c % 2 else nc.sync
+            queue.dma_start(out=out[:, c * CHUNK : (c + 1) * CHUNK], in_=res[c][:])

@@ -20,8 +20,8 @@ P = 128
 CHUNK = 256
 CHUNKS = S // CHUNK
 LOADS = (
-    ((1024, 680), (1024, 680)),
-    ((1024, 680), (512, 344), (256, 176), (256, 176)),
+    ((768, 512), (768, 512), (512, 344)),
+    ((768, 512), (640, 432), (384, 256), (256, 176)),
 )
 
 
@@ -31,17 +31,17 @@ def tile_picked_rank_none_e_kernel(tc, xT, w1_words, w1_scales, offs, out):
         sb = ctx.enter_context(tc.tile_pool(name="sb", bufs=1))
         ps = ctx.enter_context(tc.psum_pool(name="ps", bufs=1))
 
-        rows = xT.rearrange("(p j) t -> p j t", j=4)
+        rows = xT.rearrange("(p j) t -> p (j t)", j=4)
         offsets = sb.tile([P, S // 16], U16, name="offsets")
-        raw = [sb.tile([P, 2, T], F32, name=f"raw{u}") for u in range(2)]
+        raw = [sb.tile([P, 2 * T], F32, name=f"raw{u}") for u in range(2)]
         pieces = []
         for u in range(2):
-            nc.sync.dma_start(out=raw[u][:, 0, :], in_=rows[:, 2 * u, :])
-            t0 = 0
+            start, t0 = 0, 0
             for width, on_vector in LOADS[u]:
-                nc.sync.dma_start(out=raw[u][:, 1, t0 : t0 + width], in_=rows[:, 2 * u + 1, t0 : t0 + width])
+                end = T + t0 + width
+                nc.sync.dma_start(out=raw[u][:, start:end], in_=rows[:, 2 * u * T + start : 2 * u * T + end])
                 pieces.append((u, t0, width, on_vector))
-                t0 = t0 + width
+                start, t0 = end, t0 + width
             if u == 0:
                 nc.sync.dma_start(offsets[:], offs)
 
@@ -63,14 +63,15 @@ def tile_picked_rank_none_e_kernel(tc, xT, w1_words, w1_scales, offs, out):
         picked = [sb.tile([P, 2, CHUNK], U32, name=f"picked{c}") for c in range(CHUNKS)]
 
         def round_piece(u, t0, width, on_vector):
+            columns = raw[u][:].rearrange("p (e t) -> p t e", e=2)
             nc.vector.tensor_copy(
                 out=pairs[u][:, t0 : t0 + on_vector, :],
-                in_=raw[u][:, :, t0 : t0 + on_vector].rearrange("p e t -> p t e"),
+                in_=columns[:, t0 : t0 + on_vector, :],
             )
             if on_vector < width:
                 nc.scalar.activation(
                     pairs[u][:, t0 + on_vector : t0 + width, :],
-                    raw[u][:, :, t0 + on_vector : t0 + width].rearrange("p e t -> p t e"),
+                    columns[:, t0 + on_vector : t0 + width, :],
                     ACT.Copy,
                 )
 

@@ -55,25 +55,15 @@ def tile_picked_rank_none_e_kernel(tc, xT, w1_words, w1_scales, offs, out):
                 in_=w1_scales[0, 4 * q : 4 * q + 4, :].bitcast(I32),
             )
 
-        warm = sb.tile([P, 2], F32, name="warm")
-        nc.vector.memset(warm[:, 0:1], 0.0)
-        nc.scalar.activation(warm[:, 1:2], warm[:, 0:1], ACT.Exp)
-
         pairs = [sb.tile([P, T, 2], BF16, name=f"pairs{u}") for u in range(2)]
         picked = [sb.tile([P, 2, CHUNK], U32, name=f"picked{c}") for c in range(CHUNKS)]
 
         def round_piece(u, t0, width, on_vector):
-            columns = raw[u][:].rearrange("p (e t) -> p t e", e=2)
-            nc.vector.tensor_copy(
-                out=pairs[u][:, t0 : t0 + on_vector, :],
-                in_=columns[:, t0 : t0 + on_vector, :],
-            )
-            if on_vector < width:
-                nc.scalar.activation(
-                    pairs[u][:, t0 + on_vector : t0 + width, :],
-                    columns[:, t0 + on_vector : t0 + width, :],
-                    ACT.Copy,
-                )
+            rows_in = raw[u][:].rearrange("p (e c i) -> p c e i", e=2, i=4)
+            rows_out = pairs[u][:].rearrange("p (c i) e -> p c e i", i=4)
+            c0, c1, c2 = t0 // 4, (t0 + on_vector) // 4, (t0 + width) // 4
+            nc.vector.tensor_copy(out=rows_out[:, c0:c1], in_=rows_in[:, c0:c1])
+            nc.scalar.activation(rows_out[:, c1:c2], rows_in[:, c1:c2], ACT.Copy)
 
         def gather(u, c):
             window = pairs[u][:].rearrange("p t e -> p (t e)").bitcast(U32)
@@ -105,8 +95,8 @@ def tile_picked_rank_none_e_kernel(tc, xT, w1_words, w1_scales, offs, out):
 
         def weave(c):
             nc.scalar.copy(
-                woven[c][:].bitcast(U32).rearrange("p (s u) -> p s u", u=2),
-                picked[c][:].rearrange("p u s -> p s u"),
+                woven[c][:].bitcast(U32).rearrange("p (c i u) -> p c u i", u=2, i=4),
+                picked[c][:].rearrange("p u (c i) -> p c u i", i=4),
             )
 
         def product(c):

from contextlib import ExitStack

import concourse.mybir as mybir

K, T, S, N = 512, 2048, 1024, 128
FLOPS = 2 * K * S * N

F32 = mybir.dt.float32
BF16 = mybir.dt.bfloat16
I32 = mybir.dt.int32
U32 = mybir.dt.uint32
U16 = mybir.dt.uint16
U8 = mybir.dt.uint8
FP8X4 = mybir.dt.float8_e4m3fn_x4
FP4X4 = mybir.dt.float4_e2m1fn_x4
ALU = mybir.AluOpType
ACT = mybir.ActivationFunctionType

P = 128
CHUNK = 256
CHUNKS = S // CHUNK
LOADS = (
    ((768, 512), (768, 512), (512, 344)),
    ((768, 512), (640, 432), (384, 256), (256, 176)),
)


def tile_picked_rank_none_e_kernel(tc, xT, w1_words, w1_scales, offs, out):
    nc = tc.nc
    with ExitStack() as ctx:
        sb = ctx.enter_context(tc.tile_pool(name="sb", bufs=1))
        ps = ctx.enter_context(tc.psum_pool(name="ps", bufs=1))

        rows = xT.rearrange("(p j) t -> p (j t)", j=4)
        offsets = sb.tile([P, S // 16], U16, name="offsets")
        raw = [sb.tile([P, 2 * T], F32, name=f"raw{u}") for u in range(2)]
        pieces = []
        for u in range(2):
            start, t0 = 0, 0
            for width, on_vector in LOADS[u]:
                end = T + t0 + width
                nc.sync.dma_start(out=raw[u][:, start:end], in_=rows[:, 2 * u * T + start : 2 * u * T + end])
                pieces.append((u, t0, width, on_vector))
                start, t0 = end, t0 + width
            if u == 0:
                nc.sync.dma_start(offsets[:], offs)

        w_words = sb.tile([P, 2 * N], U8, name="w_words", align_bytes=64)
        w_scales = sb.tile([P, N], U8, name="w_scales", align_bytes=64)
        nc.vector.memset(w_scales[:].bitcast(I32), 0)
        nc.sync.dma_start(out=w_words[:].bitcast(I32), in_=w1_words[0].bitcast(I32))
        for q in range(4):
            nc.sync.dma_start(
                out=w_scales[32 * q : 32 * q + 4, :].bitcast(I32),
                in_=w1_scales[0, 4 * q : 4 * q + 4, :].bitcast(I32),
            )

        pairs = [sb.tile([P, T, 2], BF16, name=f"pairs{u}") for u in range(2)]
        picked = [sb.tile([P, 2, CHUNK], U32, name=f"picked{c}") for c in range(CHUNKS)]

        def round_piece(u, t0, width, on_vector):
            rows_in = raw[u][:].rearrange("p (e c i) -> p c e i", e=2, i=4)
            rows_out = pairs[u][:].rearrange("p (c i) e -> p c e i", i=4)
            c0, c1, c2 = t0 // 4, (t0 + on_vector) // 4, (t0 + width) // 4
            nc.vector.tensor_copy(out=rows_out[:, c0:c1], in_=rows_in[:, c0:c1])
            nc.scalar.activation(rows_out[:, c1:c2], rows_in[:, c1:c2], ACT.Copy)

        def gather(u, c):
            window = pairs[u][:].rearrange("p t e -> p (t e)").bitcast(U32)
            cols = CHUNK // 16
            nc.vector.tensor_copy(picked[c][:, u, :], window.indirect(offsets[:, c * cols : (c + 1) * cols]))

        for item in pieces:
            if item[0] == 0:
                round_piece(*item)
        for c in range(CHUNKS):
            gather(0, c)
        for item in pieces:
            if item[0] == 1:
                round_piece(*item)

        woven = [sb.tile([P, 4 * CHUNK], BF16, name=f"woven{c}", align_bytes=64) for c in range(CHUNKS)]
        codes = [sb.tile([P, CHUNK], U32, name=f"codes{c}", align_bytes=64) for c in range(CHUNKS)]
        scales = [sb.tile([P, CHUNK], U8, name=f"scales{c}", align_bytes=64) for c in range(CHUNKS)]
        scores = [ps.tile([P, CHUNK], F32, name=f"scores{c}") for c in range(CHUNKS)]
        expd = [sb.tile([P, CHUNK], F32, name=f"expd{c}") for c in range(CHUNKS)]
        res = [sb.tile([P, CHUNK], F32, name=f"res{c}") for c in range(CHUNKS)]
        negmax = sb.tile([P, CHUNKS], F32, name="negmax")
        negtop = sb.tile([P, 1], F32, name="negtop")
        sums = sb.tile([P, CHUNKS], F32, name="sums")
        fix = sb.tile([P, CHUNKS], F32, name="fix")
        terms = sb.tile([P, CHUNKS], F32, name="terms")
        total = sb.tile([P, 1], F32, name="total")
        inv = sb.tile([P, 1], F32, name="inv")

        def weave(c):
            nc.scalar.copy(
                woven[c][:].bitcast(U32).rearrange("p (c i u) -> p c u i", u=2, i=4),
                picked[c][:].rearrange("p u (c i) -> p c u i", i=4),
            )

        def product(c):
            nc.vector.quantize_mx(out=codes[c][:].bitcast(FP8X4), scales=scales[c][:], in_=woven[c][:])
            nc.tensor.matmul_mx(
                scores[c][:],
                lhsT=w_words[:].bitcast(FP4X4),
                lhsT_scale=w_scales[:],
                rhs=codes[c][:].bitcast(FP8X4),
                rhs_scale=scales[c][:],
                start=True,
                stop=True,
            )

        def softmax_part(c):
            nc.vector.tensor_reduce(negmax[:, c : c + 1], scores[c][:], mybir.AxisListType.X, ALU.max, negate=True)
            nc.scalar.activation(
                expd[c][:], scores[c][:], ACT.Exp, bias=negmax[:, c : c + 1], accum_out=sums[:, c : c + 1]
            )

        last = CHUNKS - 1
        for c in range(last):
            gather(1, c)
            weave(c)
        product(0)
        gather(1, last)
        weave(last)
        product(1)
        product(2)
        softmax_part(0)
        product(3)
        for c in range(1, CHUNKS):
            softmax_part(c)

        nc.vector.tensor_reduce(negtop[:], negmax[:], mybir.AxisListType.X, ALU.min)
        nc.scalar.activation(fix[:], negmax[:], ACT.Exp, bias=negtop[:], scale=-1.0)
        nc.vector.scalar_tensor_tensor(
            terms[:], sums[:], 1.0, fix[:], op0=ALU.mult, op1=ALU.mult, accum_out=total[:]
        )
        nc.vector.reciprocal(inv[:], total[:])
        for c in range(CHUNKS):
            nc.vector.tensor_scalar(
                res[c][:], expd[c][:], fix[:, c : c + 1], inv[:], op0=ALU.mult, op1=ALU.mult
            )
            queue = nc.scalar if c % 2 else nc.sync
            queue.dma_start(out=out[:, c * CHUNK : (c + 1) * CHUNK], in_=res[c][:])
